import numpy as np
import ml_dtypes


def mxq(x, axis, fmt="e4m3"):
    dtype, down = {"e4m3": (ml_dtypes.float8_e4m3fn, 7), "e5m2": (ml_dtypes.float8_e5m2, 14)}[fmt]
    v = np.moveaxis(np.asarray(x, np.float32).astype(ml_dtypes.bfloat16).astype(np.float64), axis, -1)
    blocks = v.reshape(v.shape[:-1] + (-1, 32))
    amax = np.abs(blocks).max(-1, keepdims=True)
    byte = np.maximum(np.where(amax > 0, np.frexp(amax)[1] - 1 + 127, 0) - down, 1)
    scale = np.exp2(byte - 127.0)
    codes = (blocks / scale).astype(np.float32).astype(dtype).astype(np.float64)
    return np.moveaxis((codes * scale).reshape(v.shape), -1, axis)


WIDE = False


def mx_kscale(k):
    if not WIDE:
        return np.ones(k)
    levels = np.array([10, -10, 5, -5, 0])
    if k % 512:
        return np.exp2(np.random.permutation(np.resize(levels, k // 32))).repeat(32)
    a = np.empty((k // 512, 16))
    for p in range(k // 512):
        a[p, :8] = np.random.permutation(np.resize(levels, 8))
        for g in range(8):
            far = levels[np.abs(levels - a[p, g]) >= 10]
            a[p, g + 8] = far[np.random.randint(len(far))]
    return np.exp2(a.ravel()).repeat(32)


def f64(x):
    return np.asarray(x).astype(np.float64)


def striped(idx):
    return np.tile(idx.reshape(-1, 16).T, (8, 1)).astype(np.uint16)


def unstriped(offs):
    return offs[:16].T.reshape(-1).astype(np.int64)


def striped8(idx):
    return np.concatenate([x.reshape(-1, 16).T for x in idx]).astype(np.uint16)


def runs(offs, k):
    lists = np.stack([offs[16 * r : 16 * r + 16].T.reshape(-1) for r in range(8)]).astype(np.int64)
    return lists[np.arange(k) % 512 // 64]


def pack_weight(w):
    k, n = w.shape
    w = f64(np.asarray(w, np.float32).astype(ml_dtypes.bfloat16)).reshape(k // 32, 32, n)
    amax = np.abs(w).max(1)
    byte = np.clip(np.where(amax > 0, np.frexp(amax)[1] - 1 + 127 - 7, 1), 1, 254)
    scaled = (w * np.exp2(127.0 - byte)[:, None, :]).reshape(k, n).astype(np.float32)
    words = np.ascontiguousarray(scaled.reshape(k // 512, 128, 4, n).transpose(0, 1, 3, 2)).astype(ml_dtypes.float8_e4m3fn).view(np.uint8)
    return words, np.ascontiguousarray(byte.astype(np.uint8).reshape(k // 512, 16, n))


def unpack_weight(words, scales):
    g, p, n, _ = words.shape
    vals = np.ascontiguousarray(words).view(ml_dtypes.float8_e4m3fn).astype(np.float64) * np.repeat(np.exp2(scales.astype(np.float64) - 127.0), 8, axis=1)[..., None]
    return vals.transpose(0, 1, 3, 2).reshape(g * 512, n)


def relu(v):
    return np.maximum(v, 0.0)


K, T, S, N, H = 512, 2048, 512, 512, 512


def setup_inputs():
    n = np.random.standard_normal
    s = mx_kscale(K)[:, None]
    u = mx_kscale(H)
    packed_xT = pack_weight(n((K, T)) * s)
    return {
        "x_words": packed_xT[0],
        "x_scales": packed_xT[1],
        "w1": (n((K, H)) / np.sqrt(K) / s).astype(np.float32),
        "gn": (np.random.uniform(0.5, 1.5, (H, 1)) * u[:, None]).astype(np.float32),
        "w2": (n((H, N)) / np.sqrt(H) / u[:, None]).astype(np.float32),
        "offs": striped(np.random.permutation(T)[:S]),
        "n1": striped8(np.stack([np.random.permutation(S) for _ in range(8)])),
        "n2": striped8(np.stack([np.random.permutation(S) for _ in range(8)])),
        "n3": striped8(np.stack([np.random.permutation(S) for _ in range(8)])),
        "n4": striped8(np.stack([np.random.permutation(S) for _ in range(8)])),
        "n5": striped8(np.stack([np.random.permutation(S) for _ in range(8)])),
    }


def reference(x_words, x_scales, w1, gn, w2, offs, n1, n2, n3, n4, n5):
    xq = unpack_weight(x_words, x_scales)[:, unstriped(offs)]
    y = mxq(f64(w1), 0, "e4m3").T @ xq
    z = f64(gn) * (relu(y - (y[np.arange(H)[:, None], runs(n1, H)])) + 0.5 * (relu(y[np.arange(H)[:, None], runs(n2, H)] - y)))
    h = mxq(f64(w2), 0, "e4m3").T @ mxq(z, 0, "e4m3")
    return y * (h[np.arange(N)[:, None], runs(n3, N)] - h) + 0.5 * ((y[np.arange(H)[:, None], runs(n5, H)]) * (h[np.arange(N)[:, None], runs(n4, N)] - h))

@@ -1,0 +1,233 @@
+from contextlib import ExitStack
+
+import concourse.mybir as mybir
+from concourse.masks import make_identity
+
+K, T, S, N, H = 512, 2048, 512, 512, 512
+FLOPS = 2 * K * H * S + 2 * H * N * S
+
+F32 = mybir.dt.float32
+BF16 = mybir.dt.bfloat16
+I32 = mybir.dt.int32
+U32 = mybir.dt.uint32
+U16 = mybir.dt.uint16
+U8 = mybir.dt.uint8
+FP8X4 = mybir.dt.float8_e4m3fn_x4
+ALU = mybir.AluOpType
+ACT = mybir.ActivationFunctionType
+
+P = 128
+PACK = 4
+WINDOW = 2 * S
+LAST = PACK - 1
+
+
+def tile_picked_skipflowbhinge_none_p_kernel(
+    tc, x_words, x_scales, w1, gn, w2, offs, n1, n2, n3, n4, n5, out
+):
+    nc = tc.nc
+    with ExitStack() as ctx:
+        lists = ctx.enter_context(tc.tile_pool(name="lists", bufs=1))
+        keep = ctx.enter_context(tc.tile_pool(name="keep", bufs=1))
+        psum = ctx.enter_context(tc.psum_pool(name="psum", bufs=1))
+
+        def sb(name, shape, dtype):
+            return keep.tile(shape, dtype, name=name, align_bytes=64)
+
+        def per_tile(name, shape, dtype, count=PACK):
+            return [sb("%s%d" % (name, t), shape, dtype) for t in range(count)]
+
+        offs_t = lists.tile([P, S // 16], U16, name="offs_t")
+        n1_t = lists.tile([P, S // 16], U16, name="n1_t")
+        n2_t = lists.tile([P, S // 16], U16, name="n2_t")
+        n3_t = lists.tile([P, S // 16], U16, name="n3_t")
+        n4_t = lists.tile([P, S // 16], U16, name="n4_t")
+        n5_t = lists.tile([P, S // 16], U16, name="n5_t")
+
+        xw = sb("xw", [P, T], I32)
+        xs = sb("xs", [P, T], U8)
+        xw_g = sb("xw_g", [P, S], U32)
+        xs_g = sb("xs_g", [P, S], U8)
+        w1_raw = sb("w1_raw", [P, PACK, H], F32)
+        w2_raw = sb("w2_raw", [P, PACK, N], F32)
+        w1_bf = sb("w1_bf", [P, PACK * H], BF16)
+        w2_bf = sb("w2_bf", [P, PACK * N], BF16)
+        w1_q = sb("w1_q", [P, H], U32)
+        w2_q = sb("w2_q", [P, N], U32)
+        w1_s = sb("w1_s", [P, H], U8)
+        w2_s = sb("w2_s", [P, N], U8)
+        gn_t = sb("gn_t", [P, PACK], F32)
+        neg_gn = sb("neg_gn", [P, PACK], F32)
+        ident = sb("ident", [P, P], F32)
+        y_win = per_tile("y_win", [P, WINDOW], F32)
+        h_win = per_tile("h_win", [P, WINDOW], F32)
+        y = per_tile("y", [P, S], F32)
+        d1 = per_tile("d1", [P, S], F32)
+        d2 = per_tile("d2", [P, S], F32)
+        r2 = per_tile("r2", [P, S], F32)
+        zneg = per_tile("zneg", [P, S], F32)
+        z_rows = sb("z_rows", [P, PACK, S], BF16)
+        z_bf = sb("z_bf", [P, PACK * S], BF16)
+        z_q = sb("z_q", [P, S], U32)
+        z_s = sb("z_s", [P, S], U8)
+        c = per_tile("c", [P, S], F32, LAST)
+        nch = per_tile("nch", [P, S], F32, LAST)
+        a = per_tile("a", [P, S], F32, LAST)
+        b = per_tile("b", [P, S], F32, LAST)
+        turned = per_tile("turned", [P, S], F32, LAST)
+        res = per_tile("res", [P, S], F32)
+        hh = sb("hh", [P, S], F32)
+        e3 = sb("e3", [P, S], F32)
+        e4 = sb("e4", [P, S], F32)
+        q = sb("q", [P, S], F32)
+        m = sb("m", [P, S], F32)
+        y_ps = [psum.tile([P, S], F32, name="y_ps%d" % t) for t in range(PACK)]
+        h_ps = [psum.tile([P, S], F32, name="h_ps%d" % t) for t in range(PACK)]
+
+        nc.vector.memset(xs[:].bitcast(I32), 0)
+        nc.sync.dma_start(out=gn_t[:], in_=gn.rearrange("(p t) o -> p (t o)", t=PACK))
+        nc.sync.dma_start(out=w1_raw[:], in_=w1.rearrange("(p j) c -> p j c", j=PACK))
+        nc.sync.dma_start(offs_t[:], offs)
+        for quad in range(4):
+            nc.sync.dma_start(
+                out=xs[32 * quad : 32 * quad + 4, :].bitcast(I32),
+                in_=x_scales[0, 4 * quad : 4 * quad + 4, :].bitcast(I32),
+            )
+        nc.sync.dma_start(out=xw[:], in_=x_words[0].rearrange("p n t -> p (n t)").bitcast(I32))
+        nc.sync.dma_start(n1_t[:], n1)
+        nc.sync.dma_start(n2_t[:], n2)
+        nc.sync.dma_start(out=w2_raw[:], in_=w2.rearrange("(p j) c -> p j c", j=PACK))
+        nc.sync.dma_start(n5_t[:], n5)
+        nc.sync.dma_start(n3_t[:], n3)
+        nc.sync.dma_start(n4_t[:], n4)
+
+        for t in range(PACK):
+            nc.vector.memset(y_win[t][:, S:], 0.0)
+            nc.vector.memset(h_win[t][:, S:], 0.0)
+        make_identity(nc, ident[:])
+        nc.scalar.activation(neg_gn[:], gn_t[:], ACT.Copy, scale=-1.0)
+
+        def dealt(w_bf, w_raw):
+            return (
+                w_bf[:].rearrange("p (t m j) -> p m t j", t=PACK, j=PACK),
+                w_raw[:].rearrange("p j (m t) -> p m t j", t=PACK),
+            )
+
+        dst, src = dealt(w1_bf, w1_raw)
+        nc.vector.tensor_copy(out=dst, in_=src)
+        nc.vector.quantize_mx(out=w1_q[:].bitcast(FP8X4), scales=w1_s[:], in_=w1_bf[:])
+        nc.vector.tensor_copy(xs_g[:], xs[:].indirect(offs_t[:]))
+        nc.vector.tensor_copy(xw_g[:], xw[:].bitcast(U32).indirect(offs_t[:]))
+
+        def product(ps, w_q, w_s, rhs_q, rhs_s, t):
+            cols = slice(t * P, (t + 1) * P)
+            nc.tensor.matmul_mx(
+                out=ps[:],
+                lhsT=w_q[:, cols].bitcast(FP8X4),
+                lhsT_scale=w_s[:, cols],
+                rhs=rhs_q[:].bitcast(FP8X4),
+                rhs_scale=rhs_s[:],
+                start=True,
+                stop=True,
+            )
+
+        for t in range(PACK):
+            product(y_ps[t], w1_q, w1_s, xw_g, xs_g, t)
+
+        def y_out(t):
+            nc.scalar.copy(y_win[t][:, :S], y_ps[t][:])
+            nc.scalar.copy(y[t][:], y_ps[t][:])
+
+        def z_sum(t):
+            nc.vector.scalar_tensor_tensor(zneg[t][:], d1[t][:], 0.0, r2[t][:], ALU.min, ALU.subtract)
+            nc.scalar.activation(z_rows[:, t, :], zneg[t][:], ACT.Copy, scale=neg_gn[:, t : t + 1])
+
+        dst2, src2 = dealt(w2_bf, w2_raw)
+        y_out(0)
+        for t in range(PACK):
+            if t < LAST:
+                y_out(t + 1)
+            nc.vector.tensor_tensor(d2[t][:], y_win[t][:].indirect(n2_t[:]), y[t][:], ALU.subtract)
+            nc.scalar.activation(r2[t][:], d2[t][:], ACT.Relu, scale=0.5)
+            if t > 0:
+                z_sum(t - 1)
+            nc.vector.tensor_tensor(d1[t][:], y_win[t][:].indirect(n1_t[:]), y[t][:], ALU.subtract)
+            part = slice(t * 32, (t + 1) * 32)
+            nc.scalar.copy(dst2[:, part], src2[:, part])
+
+        y5 = [d1[2][:], d1[3][:], z_bf[:].bitcast(F32)[:, :S]]
+
+        def early(t):
+            nc.vector.tensor_scalar(y5[t], y_win[t][:].indirect(n5_t[:]), 0.5, 0.0, ALU.mult, ALU.add)
+
+        def c_sum(t):
+            nc.vector.tensor_tensor(c[t][:], y5[t], y[t][:], ALU.add)
+
+        early(0)
+        z_sum(LAST)
+        nc.scalar.copy(
+            z_bf[:].rearrange("p (c i t) -> p c t i", i=4, t=PACK),
+            z_rows[:].rearrange("p t (c i) -> p c t i", i=4),
+        )
+        early(1)
+        c_sum(0)
+        nc.vector.quantize_mx(out=w2_q[:].bitcast(FP8X4), scales=w2_s[:], in_=w2_bf[:])
+        c_sum(1)
+        nc.vector.quantize_mx(out=z_q[:].bitcast(FP8X4), scales=z_s[:], in_=z_bf[:])
+        for t in range(PACK):
+            product(h_ps[t], w2_q, w2_s, z_q, z_s, t)
+        early(2)
+        c_sum(2)
+
+        out_rows = out.rearrange("(p t) s -> p t s", t=PACK)
+
+        def h_out(t):
+            if t < LAST:
+                nc.scalar.copy(h_win[t][:, :S], h_ps[t][:])
+            else:
+                nc.scalar.activation(h_win[t][:, :S], h_ps[t][:], ACT.Copy, scale=0.5)
+                nc.scalar.activation(hh[:], h_ps[t][:], ACT.Copy, scale=0.5)
+
+        def turn_add(bank, src_tile, first, last):
+            for blk in range(S // P):
+                cols = slice(blk * P, (blk + 1) * P)
+                nc.tensor.matmul(
+                    bank[:, cols],
+                    src_tile[:, cols],
+                    ident[:],
+                    start=(first and blk == 0),
+                    stop=(last and blk == S // P - 1),
+                    is_transpose=True,
+                )
+
+        for t in range(PACK):
+            h_out(t)
+        for t in range(LAST):
+            sum_bank = y_ps[t % 2]
+            back_bank = y_ps[2 + t % 2]
+            nc.vector.tensor_tensor(a[t][:], h_win[t][:].indirect(n3_t[:]), y[t][:], ALU.mult)
+            turn_add(sum_bank, a[t], True, False)
+            nc.vector.scalar_tensor_tensor(nch[t][:], h_win[t][:, :S], -1.0, c[t][:], ALU.mult, ALU.mult)
+            turn_add(sum_bank, nch[t], False, False)
+            nc.vector.tensor_tensor(b[t][:], h_win[t][:].indirect(n4_t[:]), y5[t], ALU.mult)
+            turn_add(sum_bank, b[t], False, True)
+            nc.scalar.copy(turned[t][:], sum_bank[:])
+            for blk in range(S // P):
+                cols = slice(blk * P, (blk + 1) * P)
+                nc.tensor.transpose(back_bank[:, cols], turned[t][:, cols], ident[:])
+            nc.scalar.copy(res[t][:], back_bank[:])
+            nc.sync.dma_start(out=out_rows[:, t, :], in_=res[t][:])
+
+        t = LAST
+        nc.vector.tensor_tensor(e3[:], h_win[t][:].indirect(n3_t[:]), hh[:], ALU.subtract)
+        nc.vector.tensor_tensor(e4[:], h_win[t][:].indirect(n4_t[:]), hh[:], ALU.subtract)
+        nc.vector.scalar_tensor_tensor(q[:], e3[:], 2.0, y[t][:], ALU.mult, ALU.mult)
+        half = S // 2
+        for u in range(2):
+            cols = slice(u * half, (u + 1) * half)
+            entries = slice(u * half // 16, (u + 1) * half // 16)
+            nc.vector.tensor_tensor(m[:, cols], y_win[t][:].indirect(n5_t[:, entries]), e4[:, cols], ALU.mult)
+        for u in range(2):
+            cols = slice(u * half, (u + 1) * half)
+            nc.vector.tensor_tensor(res[t][:, cols], q[:, cols], m[:, cols], ALU.add)
+            nc.sync.dma_start(out=out_rows[:, t, cols], in_=res[t][:, cols])

@@ -20,6 +20,8 @@ P = 128
 PACK = 4
 WINDOW = 2 * S
 LAST = PACK - 1
+EARLY = LAST
+HALF = S // 2
 
 
 def tile_picked_skipflowbhinge_none_p_kernel(
@@ -62,18 +64,17 @@ def tile_picked_skipflowbhinge_none_p_kernel(
         y_win = per_tile("y_win", [P, WINDOW], F32)
         h_win = per_tile("h_win", [P, WINDOW], F32)
         y = per_tile("y", [P, S], F32)
-        d1 = per_tile("d1", [P, S], F32)
+        d1 = per_tile("d1", [P, S], F32, LAST)
         d2 = per_tile("d2", [P, S], F32)
         r2 = per_tile("r2", [P, S], F32)
         zneg = per_tile("zneg", [P, S], F32)
-        z_rows = sb("z_rows", [P, PACK, S], BF16)
+        z_rows = sb("z_rows", [P, 2 * PACK - 1, HALF], BF16)
         z_bf = sb("z_bf", [P, PACK * S], BF16)
         z_q = sb("z_q", [P, S], U32)
         z_s = sb("z_s", [P, S], U8)
-        c = per_tile("c", [P, S], F32, LAST)
-        nch = per_tile("nch", [P, S], F32, LAST)
-        a = per_tile("a", [P, S], F32, LAST)
-        b = per_tile("b", [P, S], F32, LAST)
+        nch = per_tile("nch", [P, S], F32, EARLY)
+        a = per_tile("a", [P, S], F32, EARLY)
+        b = per_tile("b", [P, S], F32, EARLY)
         turned = per_tile("turned", [P, S], F32, LAST)
         res = per_tile("res", [P, S], F32)
         hh = sb("hh", [P, S], F32)
@@ -84,28 +85,35 @@ def tile_picked_skipflowbhinge_none_p_kernel(
         y_ps = [psum.tile([P, S], F32, name="y_ps%d" % t) for t in range(PACK)]
         h_ps = [psum.tile([P, S], F32, name="h_ps%d" % t) for t in range(PACK)]
 
-        nc.vector.memset(xs[:].bitcast(I32), 0)
-        nc.sync.dma_start(out=gn_t[:], in_=gn.rearrange("(p t) o -> p (t o)", t=PACK))
-        nc.sync.dma_start(out=w1_raw[:], in_=w1.rearrange("(p j) c -> p j c", j=PACK))
-        nc.sync.dma_start(offs_t[:], offs)
+        halves = [slice(0, HALF), slice(HALF, S)]
+
+        def entries(cols):
+            return slice(cols.start // 16, cols.stop // 16)
+
+        nc.gpsimd.memset(xs[:].bitcast(I32), 0)
         for quad in range(4):
-            nc.sync.dma_start(
+            nc.scalar.dma_start(
                 out=xs[32 * quad : 32 * quad + 4, :].bitcast(I32),
                 in_=x_scales[0, 4 * quad : 4 * quad + 4, :].bitcast(I32),
             )
+        nc.sync.dma_start(offs_t[:], offs)
+        w1_rows = w1.rearrange("(p j) c -> p j c", j=PACK)
+        for cols in halves:
+            nc.sync.dma_start(out=w1_raw[:, :, cols], in_=w1_rows[:, :, cols])
         nc.sync.dma_start(out=xw[:], in_=x_words[0].rearrange("p n t -> p (n t)").bitcast(I32))
-        nc.sync.dma_start(n1_t[:], n1)
+        nc.sync.dma_start(out=gn_t[:], in_=gn.rearrange("(p t) o -> p (t o)", t=PACK))
         nc.sync.dma_start(n2_t[:], n2)
+        nc.sync.dma_start(n1_t[:], n1)
         nc.sync.dma_start(out=w2_raw[:], in_=w2.rearrange("(p j) c -> p j c", j=PACK))
         nc.sync.dma_start(n5_t[:], n5)
         nc.sync.dma_start(n3_t[:], n3)
         nc.sync.dma_start(n4_t[:], n4)
 
         for t in range(PACK):
-            nc.vector.memset(y_win[t][:, S:], 0.0)
-            nc.vector.memset(h_win[t][:, S:], 0.0)
+            nc.gpsimd.memset(y_win[t][:, S:], 0.0)
+        for t in range(PACK):
+            nc.gpsimd.memset(h_win[t][:, S:], 0.0)
         make_identity(nc, ident[:])
-        nc.scalar.activation(neg_gn[:], gn_t[:], ACT.Copy, scale=-1.0)
 
         def dealt(w_bf, w_raw):
             return (
@@ -113,121 +121,156 @@ def tile_picked_skipflowbhinge_none_p_kernel(
                 w_raw[:].rearrange("p j (m t) -> p m t j", t=PACK),
             )
 
-        dst, src = dealt(w1_bf, w1_raw)
-        nc.vector.tensor_copy(out=dst, in_=src)
-        nc.vector.quantize_mx(out=w1_q[:].bitcast(FP8X4), scales=w1_s[:], in_=w1_bf[:])
         nc.vector.tensor_copy(xs_g[:], xs[:].indirect(offs_t[:]))
-        nc.vector.tensor_copy(xw_g[:], xw[:].bitcast(U32).indirect(offs_t[:]))
+        dst, src = dealt(w1_bf, w1_raw)
+        nc.scalar.copy(dst[:, : P // 2], src[:, : P // 2])
+        nc.vector.tensor_copy(out=dst[:, P // 2 :], in_=src[:, P // 2 :])
+        nc.vector.quantize_mx(out=w1_q[:].bitcast(FP8X4), scales=w1_s[:], in_=w1_bf[:])
+        nc.scalar.activation(neg_gn[:], gn_t[:], ACT.Copy, scale=-1.0)
 
-        def product(ps, w_q, w_s, rhs_q, rhs_s, t):
-            cols = slice(t * P, (t + 1) * P)
+        def product(ps, w_q, w_s, rhs_q, rhs_s, t, cols):
+            rows = slice(t * P, (t + 1) * P)
             nc.tensor.matmul_mx(
-                out=ps[:],
-                lhsT=w_q[:, cols].bitcast(FP8X4),
-                lhsT_scale=w_s[:, cols],
-                rhs=rhs_q[:].bitcast(FP8X4),
-                rhs_scale=rhs_s[:],
+                out=ps[:, cols],
+                lhsT=w_q[:, rows].bitcast(FP8X4),
+                lhsT_scale=w_s[:, rows],
+                rhs=rhs_q[:, cols].bitcast(FP8X4),
+                rhs_scale=rhs_s[:, cols],
                 start=True,
                 stop=True,
             )
 
-        for t in range(PACK):
-            product(y_ps[t], w1_q, w1_s, xw_g, xs_g, t)
+        first_banks = [y_ps[0], h_ps[0]]
+        for bank, cols in zip(first_banks, halves):
+            nc.vector.tensor_copy(xw_g[:, cols], xw[:].bitcast(U32).indirect(offs_t[:, entries(cols)]))
+            product(bank, w1_q, w1_s, xw_g, xs_g, 0, cols)
+            nc.scalar.copy(y_win[0][:, cols], bank[:, cols])
+            nc.scalar.copy(y[0][:, cols], bank[:, cols])
+        for t in range(1, PACK):
+            product(y_ps[t], w1_q, w1_s, xw_g, xs_g, t, slice(0, S))
 
         def y_out(t):
             nc.scalar.copy(y_win[t][:, :S], y_ps[t][:])
             nc.scalar.copy(y[t][:], y_ps[t][:])
 
-        def z_sum(t):
-            nc.vector.scalar_tensor_tensor(zneg[t][:], d1[t][:], 0.0, r2[t][:], ALU.min, ALU.subtract)
-            nc.scalar.activation(z_rows[:, t, :], zneg[t][:], ACT.Copy, scale=neg_gn[:, t : t + 1])
+        whole = slice(0, S)
 
-        dst2, src2 = dealt(w2_bf, w2_raw)
-        y_out(0)
-        for t in range(PACK):
-            if t < LAST:
-                y_out(t + 1)
-            nc.vector.tensor_tensor(d2[t][:], y_win[t][:].indirect(n2_t[:]), y[t][:], ALU.subtract)
-            nc.scalar.activation(r2[t][:], d2[t][:], ACT.Relu, scale=0.5)
-            if t > 0:
-                z_sum(t - 1)
-            nc.vector.tensor_tensor(d1[t][:], y_win[t][:].indirect(n1_t[:]), y[t][:], ALU.subtract)
-            part = slice(t * 32, (t + 1) * 32)
-            nc.scalar.copy(dst2[:, part], src2[:, part])
+        def row0(cols):
+            return LAST * (cols.start // HALF)
 
-        y5 = [d1[2][:], d1[3][:], z_bf[:].bitcast(F32)[:, :S]]
+        def rise(t, cols, diff):
+            nc.vector.tensor_tensor(diff, y_win[t][:].indirect(n2_t[:, entries(cols)]), y[t][:, cols], ALU.subtract)
+            nc.scalar.activation(r2[t][:, cols], diff, ACT.Relu, scale=0.5)
 
-        def early(t):
-            nc.vector.tensor_scalar(y5[t], y_win[t][:].indirect(n5_t[:]), 0.5, 0.0, ALU.mult, ALU.add)
+        def fall(t, cols, diff):
+            nc.vector.tensor_tensor(diff, y_win[t][:].indirect(n1_t[:, entries(cols)]), y[t][:, cols], ALU.subtract)
 
-        def c_sum(t):
-            nc.vector.tensor_tensor(c[t][:], y5[t], y[t][:], ALU.add)
-
-        early(0)
-        z_sum(LAST)
-        nc.scalar.copy(
-            z_bf[:].rearrange("p (c i t) -> p c t i", i=4, t=PACK),
-            z_rows[:].rearrange("p t (c i) -> p c t i", i=4),
-        )
-        early(1)
-        c_sum(0)
-        nc.vector.quantize_mx(out=w2_q[:].bitcast(FP8X4), scales=w2_s[:], in_=w2_bf[:])
-        c_sum(1)
-        nc.vector.quantize_mx(out=z_q[:].bitcast(FP8X4), scales=z_s[:], in_=z_bf[:])
-        for t in range(PACK):
-            product(h_ps[t], w2_q, w2_s, z_q, z_s, t)
-        early(2)
-        c_sum(2)
-
-        out_rows = out.rearrange("(p t) s -> p t s", t=PACK)
-
-        def h_out(t):
-            if t < LAST:
-                nc.scalar.copy(h_win[t][:, :S], h_ps[t][:])
+        def z_sum(t, cols, diff):
+            nc.vector.scalar_tensor_tensor(zneg[t][:, cols], diff, 0.0, r2[t][:, cols], ALU.min, ALU.subtract)
+            if cols == whole:
+                rows = z_rows[:, t : t + PACK : LAST, :]
+                src_rows = zneg[t][:].rearrange("p (u c) -> p u c", u=2)
             else:
-                nc.scalar.activation(h_win[t][:, :S], h_ps[t][:], ACT.Copy, scale=0.5)
-                nc.scalar.activation(hh[:], h_ps[t][:], ACT.Copy, scale=0.5)
+                rows = z_rows[:, t + row0(cols), :]
+                src_rows = zneg[t][:, cols]
+            nc.scalar.activation(rows, src_rows, ACT.Copy, scale=neg_gn[:, t : t + 1])
 
-        def turn_add(bank, src_tile, first, last):
+        def z_weave(cols):
+            nc.scalar.copy(
+                z_bf[:, PACK * cols.start : PACK * cols.stop].rearrange("p (c i t) -> p c t i", i=4, t=PACK),
+                z_rows[:, row0(cols) : row0(cols) + PACK, :].rearrange("p t (c i) -> p c t i", i=4),
+            )
+
+        def turn_add(bank, src, first_term, last_term):
             for blk in range(S // P):
                 cols = slice(blk * P, (blk + 1) * P)
                 nc.tensor.matmul(
                     bank[:, cols],
-                    src_tile[:, cols],
+                    src[:, cols],
                     ident[:],
-                    start=(first and blk == 0),
-                    stop=(last and blk == S // P - 1),
+                    start=(first_term and blk == 0),
+                    stop=(last_term and blk == S // P - 1),
                     is_transpose=True,
                 )
 
-        for t in range(PACK):
-            h_out(t)
-        for t in range(LAST):
-            sum_bank = y_ps[t % 2]
-            back_bank = y_ps[2 + t % 2]
-            nc.vector.tensor_tensor(a[t][:], h_win[t][:].indirect(n3_t[:]), y[t][:], ALU.mult)
-            turn_add(sum_bank, a[t], True, False)
-            nc.vector.scalar_tensor_tensor(nch[t][:], h_win[t][:, :S], -1.0, c[t][:], ALU.mult, ALU.mult)
-            turn_add(sum_bank, nch[t], False, False)
-            nc.vector.tensor_tensor(b[t][:], h_win[t][:].indirect(n4_t[:]), y5[t], ALU.mult)
-            turn_add(sum_bank, b[t], False, True)
-            nc.scalar.copy(turned[t][:], sum_bank[:])
+        def turn_back(sum_bank, turned_sum, back_bank):
+            nc.scalar.copy(turned_sum, sum_bank[:])
             for blk in range(S // P):
                 cols = slice(blk * P, (blk + 1) * P)
-                nc.tensor.transpose(back_bank[:, cols], turned[t][:, cols], ident[:])
-            nc.scalar.copy(res[t][:], back_bank[:])
+                nc.tensor.transpose(back_bank[:, cols], turned_sum[:, cols], ident[:])
+
+        dst2, src2 = dealt(w2_bf, w2_raw)
+        parts = [slice(0, P // 2), slice(P // 2, P)]
+        second, first = halves
+        for t in range(LAST):
+            y_out(t + 1)
+            for cols in halves if t == 0 else [whole]:
+                rise(t, cols, d2[t][:, cols])
+            if t > 0:
+                z_sum(t - 1, whole, d1[t - 1][:])
+            fall(t, whole, d1[t][:])
+            if t < len(parts):
+                nc.scalar.copy(dst2[:, parts[t]], src2[:, parts[t]])
+        prev = LAST - 1
+        y5 = [d1[prev][:], r2[LAST][:], z_bf[:].bitcast(F32)[:, :S]]
+        c_turned = z_bf[:].bitcast(F32)[:, S:]
+        c_ps = [y_ps[(t + LAST) % PACK] for t in range(EARLY)]
+
+        def early(t, cols):
+            nc.vector.tensor_scalar(
+                y5[t][:, cols], y_win[t][:].indirect(n5_t[:, entries(cols)]), 0.5, 0.0, ALU.mult, ALU.add
+            )
+
+        def c_sum(t):
+            turn_add(y_ps[t], y[t][:], True, False)
+            turn_add(y_ps[t], y5[t], False, True)
+            turn_back(y_ps[t], c_turned, c_ps[t])
+
+        rise(LAST, first, d2[LAST][:, first])
+        for cols in (first, second):
+            z_sum(prev, cols, d1[prev][:, cols])
+        fall(LAST, first, d1[prev][:, first])
+        rise(LAST, second, r2[prev][:, second])
+        z_sum(LAST, first, d1[prev][:, first])
+        z_weave(first)
+        fall(LAST, second, d1[prev][:, second])
+        nc.vector.quantize_mx(out=w2_q[:].bitcast(FP8X4), scales=w2_s[:], in_=w2_bf[:])
+        early(0, first)
+        z_sum(LAST, second, d1[prev][:, second])
+        z_weave(second)
+        early(0, second)
+        early(1, whole)
+        nc.vector.quantize_mx(out=z_q[:].bitcast(FP8X4), scales=z_s[:], in_=z_bf[:])
+        for t in range(PACK):
+            product(h_ps[t], w2_q, w2_s, z_q, z_s, t, whole)
+        early(2, whole)
+
+        out_rows = out.rearrange("(p t) s -> p t s", t=PACK)
+
+        for t in range(EARLY):
+            nc.scalar.copy(h_win[t][:, :S], h_ps[t][:])
+            c_sum(t)
+        nc.scalar.activation(h_win[LAST][:, :S], h_ps[LAST][:], ACT.Copy, scale=0.5)
+        nc.scalar.activation(hh[:], h_ps[LAST][:], ACT.Copy, scale=0.5)
+
+        for t in range(EARLY):
+            nc.vector.tensor_tensor(a[t][:], h_win[t][:].indirect(n3_t[:]), y[t][:], ALU.mult)
+            turn_add(h_ps[t], a[t][:], True, False)
+            nc.vector.tensor_tensor(b[t][:], h_win[t][:].indirect(n4_t[:]), y5[t], ALU.mult)
+            turn_add(h_ps[t], b[t][:], False, False)
+            nc.vector.scalar_tensor_tensor(nch[t][:], c_ps[t][:], -1.0, h_win[t][:, :S], ALU.mult, ALU.mult)
+            turn_add(h_ps[t], nch[t][:], False, True)
+            turn_back(h_ps[t], turned[t][:], c_ps[t])
+            nc.scalar.copy(res[t][:], c_ps[t][:])
             nc.sync.dma_start(out=out_rows[:, t, :], in_=res[t][:])
 
-        t = LAST
-        nc.vector.tensor_tensor(e3[:], h_win[t][:].indirect(n3_t[:]), hh[:], ALU.subtract)
-        nc.vector.tensor_tensor(e4[:], h_win[t][:].indirect(n4_t[:]), hh[:], ALU.subtract)
-        nc.vector.scalar_tensor_tensor(q[:], e3[:], 2.0, y[t][:], ALU.mult, ALU.mult)
-        half = S // 2
-        for u in range(2):
-            cols = slice(u * half, (u + 1) * half)
-            entries = slice(u * half // 16, (u + 1) * half // 16)
-            nc.vector.tensor_tensor(m[:, cols], y_win[t][:].indirect(n5_t[:, entries]), e4[:, cols], ALU.mult)
-        for u in range(2):
-            cols = slice(u * half, (u + 1) * half)
-            nc.vector.tensor_tensor(res[t][:, cols], q[:, cols], m[:, cols], ALU.add)
-            nc.sync.dma_start(out=out_rows[:, t, cols], in_=res[t][:, cols])
+        nc.vector.tensor_tensor(e3[:], h_win[LAST][:].indirect(n3_t[:]), hh[:], ALU.subtract)
+        nc.vector.tensor_tensor(e4[:], h_win[LAST][:].indirect(n4_t[:]), hh[:], ALU.subtract)
+        nc.vector.scalar_tensor_tensor(q[:], e3[:], 2.0, y[LAST][:], ALU.mult, ALU.mult)
+        for cols in halves:
+            nc.vector.tensor_tensor(
+                m[:, cols], y_win[LAST][:].indirect(n5_t[:, entries(cols)]), e4[:, cols], ALU.mult
+            )
+        for cols in halves:
+            nc.vector.tensor_tensor(res[LAST][:, cols], q[:, cols], m[:, cols], ALU.add)
+            nc.sync.dma_start(out=out_rows[:, LAST, cols], in_=res[LAST][:, cols])

@@ -90,7 +90,7 @@ def tile_picked_skipflowbhinge_none_p_kernel(
         def entries(cols):
             return slice(cols.start // 16, cols.stop // 16)
 
-        nc.gpsimd.memset(xs[:].bitcast(I32), 0)
+        nc.vector.memset(xs[:].bitcast(I32), 0)
         for quad in range(4):
             nc.scalar.dma_start(
                 out=xs[32 * quad : 32 * quad + 4, :].bitcast(I32),
@@ -110,9 +110,9 @@ def tile_picked_skipflowbhinge_none_p_kernel(
         nc.sync.dma_start(n4_t[:], n4)
 
         for t in range(PACK):
-            nc.gpsimd.memset(y_win[t][:, S:], 0.0)
+            nc.vector.memset(y_win[t][:, S:], 0.0)
         for t in range(PACK):
-            nc.gpsimd.memset(h_win[t][:, S:], 0.0)
+            nc.vector.memset(h_win[t][:, S:], 0.0)
         make_identity(nc, ident[:])
 
         def dealt(w_bf, w_raw):
@@ -212,7 +212,7 @@ def tile_picked_skipflowbhinge_none_p_kernel(
             if t < len(parts):
                 nc.scalar.copy(dst2[:, parts[t]], src2[:, parts[t]])
         prev = LAST - 1
-        y5 = [d1[prev][:], r2[LAST][:], z_bf[:].bitcast(F32)[:, :S]]
+        y5 = [r2[LAST][:], d1[prev][:], z_bf[:].bitcast(F32)[:, :S]]
         c_turned = z_bf[:].bitcast(F32)[:, S:]
         c_ps = [y_ps[(t + LAST) % PACK] for t in range(EARLY)]
 
@@ -233,10 +233,10 @@ def tile_picked_skipflowbhinge_none_p_kernel(
         rise(LAST, second, r2[prev][:, second])
         z_sum(LAST, first, d1[prev][:, first])
         z_weave(first)
-        fall(LAST, second, d1[prev][:, second])
+        fall(LAST, second, d1[prev][:, first])
         nc.vector.quantize_mx(out=w2_q[:].bitcast(FP8X4), scales=w2_s[:], in_=w2_bf[:])
         early(0, first)
-        z_sum(LAST, second, d1[prev][:, second])
+        z_sum(LAST, second, d1[prev][:, first])
         z_weave(second)
         early(0, second)
         early(1, whole)

from contextlib import ExitStack

import concourse.mybir as mybir
from concourse.masks import make_identity

K, T, S, N, H = 512, 2048, 512, 512, 512
FLOPS = 2 * K * H * S + 2 * H * N * S

F32 = mybir.dt.float32
BF16 = mybir.dt.bfloat16
I32 = mybir.dt.int32
U32 = mybir.dt.uint32
U16 = mybir.dt.uint16
U8 = mybir.dt.uint8
FP8X4 = mybir.dt.float8_e4m3fn_x4
ALU = mybir.AluOpType
ACT = mybir.ActivationFunctionType

P = 128
PACK = 4
WINDOW = 2 * S
LAST = PACK - 1
EARLY = LAST
HALF = S // 2


def tile_picked_skipflowbhinge_none_p_kernel(
    tc, x_words, x_scales, w1, gn, w2, offs, n1, n2, n3, n4, n5, out
):
    nc = tc.nc
    with ExitStack() as ctx:
        lists = ctx.enter_context(tc.tile_pool(name="lists", bufs=1))
        keep = ctx.enter_context(tc.tile_pool(name="keep", bufs=1))
        psum = ctx.enter_context(tc.psum_pool(name="psum", bufs=1))

        def sb(name, shape, dtype):
            return keep.tile(shape, dtype, name=name, align_bytes=64)

        def per_tile(name, shape, dtype, count=PACK):
            return [sb("%s%d" % (name, t), shape, dtype) for t in range(count)]

        offs_t = lists.tile([P, S // 16], U16, name="offs_t")
        n1_t = lists.tile([P, S // 16], U16, name="n1_t")
        n2_t = lists.tile([P, S // 16], U16, name="n2_t")
        n3_t = lists.tile([P, S // 16], U16, name="n3_t")
        n4_t = lists.tile([P, S // 16], U16, name="n4_t")
        n5_t = lists.tile([P, S // 16], U16, name="n5_t")

        xw = sb("xw", [P, T], I32)
        xs = sb("xs", [P, T], U8)
        xw_g = sb("xw_g", [P, S], U32)
        xs_g = sb("xs_g", [P, S], U8)
        w1_raw = sb("w1_raw", [P, PACK, H], F32)
        w2_raw = sb("w2_raw", [P, PACK, N], F32)
        w1_bf = sb("w1_bf", [P, PACK * H], BF16)
        w2_bf = sb("w2_bf", [P, PACK * N], BF16)
        w1_q = sb("w1_q", [P, H], U32)
        w2_q = sb("w2_q", [P, N], U32)
        w1_s = sb("w1_s", [P, H], U8)
        w2_s = sb("w2_s", [P, N], U8)
        gn_t = sb("gn_t", [P, PACK], F32)
        neg_gn = sb("neg_gn", [P, PACK], F32)
        ident = sb("ident", [P, P], F32)
        y_win = per_tile("y_win", [P, WINDOW], F32)
        h_win = per_tile("h_win", [P, WINDOW], F32)
        y = per_tile("y", [P, S], F32)
        d1 = per_tile("d1", [P, S], F32, LAST)
        d2 = per_tile("d2", [P, S], F32)
        r2 = per_tile("r2", [P, S], F32)
        zneg = per_tile("zneg", [P, S], F32)
        z_rows = sb("z_rows", [P, 2 * PACK - 1, HALF], BF16)
        z_bf = sb("z_bf", [P, PACK * S], BF16)
        z_q = sb("z_q", [P, S], U32)
        z_s = sb("z_s", [P, S], U8)
        nch = per_tile("nch", [P, S], F32, EARLY)
        a = per_tile("a", [P, S], F32, EARLY)
        b = per_tile("b", [P, S], F32, EARLY)
        turned = per_tile("turned", [P, S], F32, LAST)
        res = per_tile("res", [P, S], F32)
        hh = sb("hh", [P, S], F32)
        e3 = sb("e3", [P, S], F32)
        e4 = sb("e4", [P, S], F32)
        q = sb("q", [P, S], F32)
        m = sb("m", [P, S], F32)
        y_ps = [psum.tile([P, S], F32, name="y_ps%d" % t) for t in range(PACK)]
        h_ps = [psum.tile([P, S], F32, name="h_ps%d" % t) for t in range(PACK)]

        halves = [slice(0, HALF), slice(HALF, S)]

        def entries(cols):
            return slice(cols.start // 16, cols.stop // 16)

        nc.vector.memset(xs[:].bitcast(I32), 0)
        for quad in range(4):
            nc.scalar.dma_start(
                out=xs[32 * quad : 32 * quad + 4, :].bitcast(I32),
                in_=x_scales[0, 4 * quad : 4 * quad + 4, :].bitcast(I32),
            )
        nc.sync.dma_start(offs_t[:], offs)
        w1_rows = w1.rearrange("(p j) c -> p j c", j=PACK)
        for cols in halves:
            nc.sync.dma_start(out=w1_raw[:, :, cols], in_=w1_rows[:, :, cols])
        nc.sync.dma_start(out=xw[:], in_=x_words[0].rearrange("p n t -> p (n t)").bitcast(I32))
        nc.sync.dma_start(out=gn_t[:], in_=gn.rearrange("(p t) o -> p (t o)", t=PACK))
        nc.sync.dma_start(n2_t[:], n2)
        nc.sync.dma_start(n1_t[:], n1)
        nc.sync.dma_start(out=w2_raw[:], in_=w2.rearrange("(p j) c -> p j c", j=PACK))
        nc.sync.dma_start(n5_t[:], n5)
        nc.sync.dma_start(n3_t[:], n3)
        nc.sync.dma_start(n4_t[:], n4)

        for t in range(PACK):
            nc.vector.memset(y_win[t][:, S:], 0.0)
        for t in range(PACK):
            nc.vector.memset(h_win[t][:, S:], 0.0)
        make_identity(nc, ident[:])

        def dealt(w_bf, w_raw):
            return (
                w_bf[:].rearrange("p (t m j) -> p m t j", t=PACK, j=PACK),
                w_raw[:].rearrange("p j (m t) -> p m t j", t=PACK),
            )

        nc.vector.tensor_copy(xs_g[:], xs[:].indirect(offs_t[:]))
        dst, src = dealt(w1_bf, w1_raw)
        nc.scalar.copy(dst[:, : P // 2], src[:, : P // 2])
        nc.vector.tensor_copy(out=dst[:, P // 2 :], in_=src[:, P // 2 :])
        nc.vector.quantize_mx(out=w1_q[:].bitcast(FP8X4), scales=w1_s[:], in_=w1_bf[:])
        nc.scalar.activation(neg_gn[:], gn_t[:], ACT.Copy, scale=-1.0)

        def product(ps, w_q, w_s, rhs_q, rhs_s, t, cols):
            rows = slice(t * P, (t + 1) * P)
            nc.tensor.matmul_mx(
                out=ps[:, cols],
                lhsT=w_q[:, rows].bitcast(FP8X4),
                lhsT_scale=w_s[:, rows],
                rhs=rhs_q[:, cols].bitcast(FP8X4),
                rhs_scale=rhs_s[:, cols],
                start=True,
                stop=True,
            )

        first_banks = [y_ps[0], h_ps[0]]
        for bank, cols in zip(first_banks, halves):
            nc.vector.tensor_copy(xw_g[:, cols], xw[:].bitcast(U32).indirect(offs_t[:, entries(cols)]))
            product(bank, w1_q, w1_s, xw_g, xs_g, 0, cols)
            nc.scalar.copy(y_win[0][:, cols], bank[:, cols])
            nc.scalar.copy(y[0][:, cols], bank[:, cols])
        for t in range(1, PACK):
            product(y_ps[t], w1_q, w1_s, xw_g, xs_g, t, slice(0, S))

        def y_out(t):
            nc.scalar.copy(y_win[t][:, :S], y_ps[t][:])
            nc.scalar.copy(y[t][:], y_ps[t][:])

        whole = slice(0, S)

        def row0(cols):
            return LAST * (cols.start // HALF)

        def rise(t, cols, diff):
            nc.vector.tensor_tensor(diff, y_win[t][:].indirect(n2_t[:, entries(cols)]), y[t][:, cols], ALU.subtract)
            nc.scalar.activation(r2[t][:, cols], diff, ACT.Relu, scale=0.5)

        def fall(t, cols, diff):
            nc.vector.tensor_tensor(diff, y_win[t][:].indirect(n1_t[:, entries(cols)]), y[t][:, cols], ALU.subtract)

        def z_sum(t, cols, diff):
            nc.vector.scalar_tensor_tensor(zneg[t][:, cols], diff, 0.0, r2[t][:, cols], ALU.min, ALU.subtract)
            if cols == whole:
                rows = z_rows[:, t : t + PACK : LAST, :]
                src_rows = zneg[t][:].rearrange("p (u c) -> p u c", u=2)
            else:
                rows = z_rows[:, t + row0(cols), :]
                src_rows = zneg[t][:, cols]
            nc.scalar.activation(rows, src_rows, ACT.Copy, scale=neg_gn[:, t : t + 1])

        def z_weave(cols):
            nc.scalar.copy(
                z_bf[:, PACK * cols.start : PACK * cols.stop].rearrange("p (c i t) -> p c t i", i=4, t=PACK),
                z_rows[:, row0(cols) : row0(cols) + PACK, :].rearrange("p t (c i) -> p c t i", i=4),
            )

        def turn_add(bank, src, first_term, last_term):
            for blk in range(S // P):
                cols = slice(blk * P, (blk + 1) * P)
                nc.tensor.matmul(
                    bank[:, cols],
                    src[:, cols],
                    ident[:],
                    start=(first_term and blk == 0),
                    stop=(last_term and blk == S // P - 1),
                    is_transpose=True,
                )

        def turn_back(sum_bank, turned_sum, back_bank):
            nc.scalar.copy(turned_sum, sum_bank[:])
            for blk in range(S // P):
                cols = slice(blk * P, (blk + 1) * P)
                nc.tensor.transpose(back_bank[:, cols], turned_sum[:, cols], ident[:])

        dst2, src2 = dealt(w2_bf, w2_raw)
        parts = [slice(0, P // 2), slice(P // 2, P)]
        second, first = halves
        for t in range(LAST):
            y_out(t + 1)
            for cols in halves if t == 0 else [whole]:
                rise(t, cols, d2[t][:, cols])
            if t > 0:
                z_sum(t - 1, whole, d1[t - 1][:])
            fall(t, whole, d1[t][:])
            if t < len(parts):
                nc.scalar.copy(dst2[:, parts[t]], src2[:, parts[t]])
        prev = LAST - 1
        y5 = [r2[LAST][:], d1[prev][:], z_bf[:].bitcast(F32)[:, :S]]
        c_turned = z_bf[:].bitcast(F32)[:, S:]
        c_ps = [y_ps[(t + LAST) % PACK] for t in range(EARLY)]

        def early(t, cols):
            nc.vector.tensor_scalar(
                y5[t][:, cols], y_win[t][:].indirect(n5_t[:, entries(cols)]), 0.5, 0.0, ALU.mult, ALU.add
            )

        def c_sum(t):
            turn_add(y_ps[t], y[t][:], True, False)
            turn_add(y_ps[t], y5[t], False, True)
            turn_back(y_ps[t], c_turned, c_ps[t])

        rise(LAST, first, d2[LAST][:, first])
        for cols in (first, second):
            z_sum(prev, cols, d1[prev][:, cols])
        fall(LAST, first, d1[prev][:, first])
        rise(LAST, second, r2[prev][:, second])
        z_sum(LAST, first, d1[prev][:, first])
        z_weave(first)
        fall(LAST, second, d1[prev][:, first])
        nc.vector.quantize_mx(out=w2_q[:].bitcast(FP8X4), scales=w2_s[:], in_=w2_bf[:])
        early(0, first)
        z_sum(LAST, second, d1[prev][:, first])
        z_weave(second)
        early(0, second)
        early(1, whole)
        nc.vector.quantize_mx(out=z_q[:].bitcast(FP8X4), scales=z_s[:], in_=z_bf[:])
        for t in range(PACK):
            product(h_ps[t], w2_q, w2_s, z_q, z_s, t, whole)
        early(2, whole)

        out_rows = out.rearrange("(p t) s -> p t s", t=PACK)

        for t in range(EARLY):
            nc.scalar.copy(h_win[t][:, :S], h_ps[t][:])
            c_sum(t)
        nc.scalar.activation(h_win[LAST][:, :S], h_ps[LAST][:], ACT.Copy, scale=0.5)
        nc.scalar.activation(hh[:], h_ps[LAST][:], ACT.Copy, scale=0.5)

        for t in range(EARLY):
            nc.vector.tensor_tensor(a[t][:], h_win[t][:].indirect(n3_t[:]), y[t][:], ALU.mult)
            turn_add(h_ps[t], a[t][:], True, False)
            nc.vector.tensor_tensor(b[t][:], h_win[t][:].indirect(n4_t[:]), y5[t], ALU.mult)
            turn_add(h_ps[t], b[t][:], False, False)
            nc.vector.scalar_tensor_tensor(nch[t][:], c_ps[t][:], -1.0, h_win[t][:, :S], ALU.mult, ALU.mult)
            turn_add(h_ps[t], nch[t][:], False, True)
            turn_back(h_ps[t], turned[t][:], c_ps[t])
            nc.scalar.copy(res[t][:], c_ps[t][:])
            nc.sync.dma_start(out=out_rows[:, t, :], in_=res[t][:])

        nc.vector.tensor_tensor(e3[:], h_win[LAST][:].indirect(n3_t[:]), hh[:], ALU.subtract)
        nc.vector.tensor_tensor(e4[:], h_win[LAST][:].indirect(n4_t[:]), hh[:], ALU.subtract)
        nc.vector.scalar_tensor_tensor(q[:], e3[:], 2.0, y[LAST][:], ALU.mult, ALU.mult)
        for cols in halves:
            nc.vector.tensor_tensor(
                m[:, cols], y_win[LAST][:].indirect(n5_t[:, entries(cols)]), e4[:, cols], ALU.mult
            )
        for cols in halves:
            nc.vector.tensor_tensor(res[LAST][:, cols], q[:, cols], m[:, cols], ALU.add)
            nc.sync.dma_start(out=out_rows[:, LAST, cols], in_=res[LAST][:, cols])
